import numpy as np
import ml_dtypes


def mxq(x, axis, fmt="e4m3"):
    dtype, down = {"e4m3": (ml_dtypes.float8_e4m3fn, 7), "e5m2": (ml_dtypes.float8_e5m2, 14)}[fmt]
    v = np.moveaxis(np.asarray(x, np.float32).astype(ml_dtypes.bfloat16).astype(np.float64), axis, -1)
    blocks = v.reshape(v.shape[:-1] + (-1, 32))
    amax = np.abs(blocks).max(-1, keepdims=True)
    byte = np.maximum(np.where(amax > 0, np.frexp(amax)[1] - 1 + 127, 0) - down, 1)
    scale = np.exp2(byte - 127.0)
    codes = (blocks / scale).astype(np.float32).astype(dtype).astype(np.float64)
    return np.moveaxis((codes * scale).reshape(v.shape), -1, axis)


WIDE = False


def mx_kscale(k):
    if not WIDE:
        return np.ones(k)
    levels = np.array([10, -10, 5, -5, 0])
    if k % 512:
        return np.exp2(np.random.permutation(np.resize(levels, k // 32))).repeat(32)
    a = np.empty((k // 512, 16))
    for p in range(k // 512):
        a[p, :8] = np.random.permutation(np.resize(levels, 8))
        for g in range(8):
            far = levels[np.abs(levels - a[p, g]) >= 10]
            a[p, g + 8] = far[np.random.randint(len(far))]
    return np.exp2(a.ravel()).repeat(32)


def f64(x):
    return np.asarray(x).astype(np.float64)


def striped(idx):
    return np.tile(idx.reshape(-1, 16).T, (8, 1)).astype(np.uint16)


def unstriped(offs):
    return offs[:16].T.reshape(-1).astype(np.int64)


def striped8(idx):
    return np.concatenate([x.reshape(-1, 16).T for x in idx]).astype(np.uint16)


def runs(offs, k):
    lists = np.stack([offs[16 * r : 16 * r + 16].T.reshape(-1) for r in range(8)]).astype(np.int64)
    return lists[np.arange(k) % 512 // 64]


def pack_weight(w):
    k, n = w.shape
    w = f64(np.asarray(w, np.float32).astype(ml_dtypes.bfloat16)).reshape(k // 32, 32, n)
    amax = np.abs(w).max(1)
    byte = np.clip(np.where(amax > 0, np.frexp(amax)[1] - 1 + 127 - 7, 1), 1, 254)
    scaled = (w * np.exp2(127.0 - byte)[:, None, :]).reshape(k, n).astype(np.float32)
    words = np.ascontiguousarray(scaled.reshape(k // 512, 128, 4, n).transpose(0, 1, 3, 2)).astype(ml_dtypes.float8_e4m3fn).view(np.uint8)
    return words, np.ascontiguousarray(byte.astype(np.uint8).reshape(k // 512, 16, n))


def unpack_weight(words, scales):
    g, p, n, _ = words.shape
    vals = np.ascontiguousarray(words).view(ml_dtypes.float8_e4m3fn).astype(np.float64) * np.repeat(np.exp2(scales.astype(np.float64) - 127.0), 8, axis=1)[..., None]
    return vals.transpose(0, 1, 3, 2).reshape(g * 512, n)


K, T, S, N, G, H = 512, 2048, 512, 512, 2048, 512


def setup_inputs():
    n = np.random.standard_normal
    s = mx_kscale(K)[:, None]
    u = mx_kscale(S)
    packed_xT = pack_weight(n((K, T)) * s)
    packed_dT = pack_weight(n((K, G)) / s)
    return {
        "x_words": packed_xT[0],
        "x_scales": packed_xT[1],
        "d_words": packed_dT[0],
        "d_scales": packed_dT[1],
        "gn": (np.random.uniform(0.5, 1.5, (H, 1)) * u[:, None]).astype(np.float32),
        "w1": (n((H, N)) / np.sqrt(H) / u[:, None]).astype(np.float32),
        "offs": striped(np.random.permutation(T)[:S]),
        "k1": striped8(np.random.randint(0, G, (8, H))),
        "two": striped(np.random.permutation(T)[:S]),
        "n1": striped(np.random.permutation(S)),
        "n2": striped(np.random.permutation(S)),
        "n3": striped8(np.stack([np.random.permutation(S) for _ in range(8)])),
    }


def reference(x_words, x_scales, d_words, d_scales, gn, w1, offs, k1, two, n1, n2, n3):
    d_k1 = unpack_weight(d_words, d_scales)[np.arange(K)[:, None], runs(k1, K)]
    xq = unpack_weight(x_words, x_scales)[:, unstriped(offs)]
    a = 0.0625 * (d_k1.T @ xq)
    x_two = unpack_weight(x_words, x_scales)[:, unstriped(two)]
    b = 0.0625 * (d_k1.T @ x_two)
    z = f64(gn) * (a * (np.tanh(b[:, unstriped(n1)] - b[:, unstriped(n2)])))
    h = mxq(f64(w1), 0, "e4m3").T @ mxq(z, 0, "e4m3")
    pa = h[np.arange(N)[:, None], runs(n3, N)]
    return (2.0 * (h * pa)) / ((h) ** 2 + (pa) ** 2 + 0.5)

@@ -1,0 +1,327 @@
+from contextlib import ExitStack
+
+import concourse.mybir as mybir
+from concourse.masks import make_identity
+
+K, T, S, N, G, H = 512, 2048, 512, 512, 2048, 512
+FLOPS = 2 * K * H * S * 2 + 2 * H * N * S
+
+F32 = mybir.dt.float32
+BF16 = mybir.dt.bfloat16
+I32 = mybir.dt.int32
+U32 = mybir.dt.uint32
+U16 = mybir.dt.uint16
+U8 = mybir.dt.uint8
+FP8X4 = mybir.dt.float8_e4m3fn_x4
+ACT = mybir.ActivationFunctionType
+ALU = mybir.AluOpType
+
+P = 128
+PACK = 4
+PARTS = [(0, 256), (256, 512)]
+PASSES = [[(0, 256)], [(256, 512)]]
+
+
+def tile_picked_twksjointbharm_none_p_kernel(
+    tc, x_words, x_scales, d_words, d_scales, gn, w1, offs, k1, two, n1, n2, n3, out
+):
+    nc = tc.nc
+    with ExitStack() as ctx:
+        lists = ctx.enter_context(tc.tile_pool(name="lists", bufs=1))
+        keep = ctx.enter_context(tc.tile_pool(name="keep", bufs=1))
+        psum = ctx.enter_context(tc.psum_pool(name="psum", bufs=1))
+
+        def load_list(name, src):
+            tile = lists.tile([P, S // 16], U16, name=name)
+            nc.sync.dma_start(tile[:], src)
+            return tile
+
+        def tiles(name, dtype=F32):
+            return [keep.tile([P, S], dtype, name=f"{name}{t}") for t in range(PACK)]
+
+        d_byte_table = keep.tile([P, G], U8, name="d_byte_table", align_bytes=64)
+        x_byte_table = keep.tile([P, T], U8, name="x_byte_table", align_bytes=64)
+        d_word_table = keep.tile([P, G], U32, name="d_word_table", align_bytes=64)
+        x_word_table = keep.tile([P, T], U32, name="x_word_table", align_bytes=64)
+        key_scales = keep.tile([P, H], U8, name="key_scales", align_bytes=64)
+        w_raw = keep.tile([P, PACK, N], F32, name="w_raw")
+        gain = keep.tile([P, PACK], F32, name="gain")
+        nc.gpsimd.memset(d_byte_table[:].bitcast(I32), 0)
+        nc.vector.memset(x_byte_table[:].bitcast(I32), 0)
+        nc.gpsimd.memset(key_scales[:].bitcast(I32), 0)
+        loads = {
+            "d": (d_word_table[:].bitcast(I32), d_words[0].rearrange("p n t -> p (n t)").bitcast(I32)),
+            "x": (x_word_table[:].bitcast(I32), x_words[0].rearrange("p n t -> p (n t)").bitcast(I32)),
+            "w": (w_raw[:], w1.rearrange("(p j) m -> p j m", j=PACK)),
+        }
+
+        def load_x_bytes(q):
+            nc.sync.dma_start(
+                x_byte_table[32 * q : 32 * q + 4, :].bitcast(I32), x_scales[0][4 * q : 4 * q + 4, :].bitcast(I32)
+            )
+
+        k1_list = load_list("k1_list", k1)
+        d_rows = d_scales[0].rearrange("(r s) n -> s r n", s=2)
+        for s in range(2):
+            nc.sync.dma_start(d_byte_table[s:P:16, :].bitcast(I32), d_rows[s].bitcast(I32))
+        two_list = load_list("two_list", two)
+        offs_list = load_list("offs_list", offs)
+        load_x_bytes(0)
+        load_x_bytes(1)
+        nc.sync.dma_start(*loads["d"])
+        load_x_bytes(2)
+        load_x_bytes(3)
+        n2_list = load_list("n2_list", n2)
+        n1_list = load_list("n1_list", n1)
+        nc.sync.dma_start(*loads["w"])
+        nc.sync.dma_start(*loads["x"])
+        n3_list = load_list("n3_list", n3)
+        nc.gpsimd.dma_start(gain[:], gn.rearrange("(p t) o -> p (t o)", t=PACK))
+
+        gain16 = keep.tile([P, PACK], F32, name="gain16")
+        nc.gpsimd.tensor_scalar(gain16[:], gain[:], 0.0625, 0.0, ALU.mult, ALU.add)
+        identity = keep.tile([P, P], F32, name="identity")
+        make_identity(nc, identity[:])
+        half = keep.tile([P, 1], F32, name="half")
+        nc.gpsimd.memset(half[:], 0.5)
+
+        def gather(name, table, offsets, dtype):
+            tile = keep.tile([P, S], dtype, name=name, align_bytes=64)
+            nc.vector.tensor_copy(tile[:], table[:].indirect(offsets[:]))
+            return tile
+
+        key_bytes = gather("key_bytes", d_byte_table, k1_list, U8)
+        key_bytes_dealt = keep.tile([P, H], U8, name="key_bytes_dealt", align_bytes=64)
+        nc.vector.tensor_copy(
+            key_bytes_dealt[:].rearrange("p (t m) -> p t m", t=PACK),
+            key_bytes[:].rearrange("p (m t) -> p t m", t=PACK),
+        )
+        for r in range(4):
+            src = 16 * (r // 2) + r % 2
+            nc.scalar.dma_start(key_scales[r:P:32, :].bitcast(I32), key_bytes_dealt[src:P:32, :].bitcast(I32))
+        key_words = gather("key_words", d_word_table, k1_list, U32)
+        key_codes = keep.tile([P, H], U32, name="key_codes", align_bytes=64)
+        nc.vector.tensor_copy(
+            key_codes[:].rearrange("p (t m) -> p m t", t=PACK),
+            key_words[:].rearrange("p (m t) -> p m t", t=PACK),
+        )
+        b_scales = gather("b_scales", x_byte_table, two_list, U8)
+        a_scales = gather("a_scales", x_byte_table, offs_list, U8)
+        b_codes = gather("b_codes", x_word_table, two_list, U32)
+        a_codes = gather("a_codes", x_word_table, offs_list, U32)
+
+        def product(bank, lhs_codes, lhs_scales, t, rhs_codes, rhs_scales, cols):
+            rows = slice(t * P, (t + 1) * P)
+            nc.tensor.matmul_mx(
+                out=bank[:, cols],
+                lhsT=lhs_codes[:, rows].bitcast(FP8X4),
+                lhsT_scale=lhs_scales[:, rows],
+                rhs=rhs_codes[:, cols].bitcast(FP8X4),
+                rhs_scale=rhs_scales[:, cols],
+                start=True,
+                stop=True,
+            )
+
+        b_banks = [psum.tile([P, S], F32, name=f"b{t}", tag=f"bank{t}") for t in range(PACK)]
+        a_banks = [psum.tile([P, S], F32, name=f"a{t}", tag=f"bank{4 + t}") for t in range(PACK)]
+        for t in range(PACK):
+            product(b_banks[t], key_codes, key_scales, t, b_codes, b_scales, slice(0, S))
+        for t in range(PACK):
+            product(a_banks[t], key_codes, key_scales, t, a_codes, a_scales, slice(0, S))
+
+        z_rows = keep.tile([P, PACK, S], BF16, name="z_rows", align_bytes=64)
+        w_grouped = keep.tile([P, N * PACK], BF16, name="w_grouped", align_bytes=64)
+        w_out = w_grouped[:].rearrange("p (t m j) -> p m j t", t=PACK, j=PACK)
+        w_in = w_raw[:].rearrange("p j (m t) -> p m j t", t=PACK)
+        w_codes = keep.tile([P, N], U32, name="w_codes", align_bytes=64)
+        w_scales = keep.tile([P, N], U8, name="w_scales", align_bytes=64)
+        z_grouped = keep.tile([P, S, PACK], BF16, name="z_grouped", align_bytes=64)
+        z_codes = keep.tile([P, S], U32, name="z_codes", align_bytes=64)
+        z_scales = keep.tile([P, S], U8, name="z_scales", align_bytes=64)
+        b_windows = tiles("b_window")
+        minus_b2 = tiles("minus_b2_")
+        diff = tiles("diff")
+        squash = tiles("squash")
+        h_windows = tiles("h_window")
+        partner = tiles("partner")
+        h_sq = tiles("h_sq")
+        partner_sq = tiles("partner_sq")
+        denom = tiles("denom")
+        root = tiles("root")
+        inverse = tiles("inverse")
+        numer = tiles("numer")
+        result = tiles("result")
+        out_rows = out.rearrange("(p t) j -> p t j", t=PACK)
+        h_banks = []
+
+        def entries(offsets, lo, hi):
+            return offsets[:, lo // 16 : hi // 16]
+
+        def copy_b(t):
+            nc.scalar.copy(b_windows[t][:], b_banks[t][:])
+
+        def fetch_b2(t, lo, hi):
+            nc.scalar.activation(
+                minus_b2[t][:, lo:hi], b_windows[t][:].indirect(entries(n2_list, lo, hi)), ACT.Copy, scale=-1.0
+            )
+
+        def fetch_b1(t, lo, hi):
+            nc.vector.tensor_tensor(
+                diff[t][:, lo:hi], b_windows[t][:].indirect(entries(n1_list, lo, hi)), minus_b2[t][:, lo:hi], ALU.add
+            )
+
+        def tanh(t, lo, hi):
+            nc.scalar.activation(squash[t][:, lo:hi], diff[t][:, lo:hi], ACT.Tanh, scale=0.0625)
+
+        def gate(t, lo, hi):
+            nc.vector.scalar_tensor_tensor(
+                z_rows[:, t, lo:hi], a_banks[t][:, lo:hi], gain16[:, t : t + 1], squash[t][:, lo:hi], ALU.mult, ALU.mult
+            )
+
+        def cast_w(q, engine, n=4):
+            rows = slice(q * P // n, (q + 1) * P // n)
+            if engine == "s":
+                nc.scalar.copy(w_out[:, rows], w_in[:, rows])
+            else:
+                nc.vector.tensor_copy(w_out[:, rows], w_in[:, rows])
+
+        def quant_w():
+            nc.vector.quantize_mx(out=w_codes[:].bitcast(FP8X4), scales=w_scales[:], in_=w_grouped[:])
+
+        def weave(lo, hi):
+            nc.vector.tensor_copy(
+                z_grouped[:, lo:hi, :].rearrange("p (c i) t -> p c t i", i=4),
+                z_rows[:, :, lo:hi].rearrange("p t (c i) -> p c t i", i=4),
+            )
+
+        def quant_z(lo, hi):
+            nc.vector.quantize_mx(
+                out=z_codes[:, lo:hi].bitcast(FP8X4),
+                scales=z_scales[:, lo:hi],
+                in_=z_grouped[:, lo:hi, :].rearrange("p j t -> p (j t)"),
+            )
+
+        def product_h(t, part):
+            if part == 0:
+                h_banks.append(psum.tile([P, S], F32, name=f"h{t}", tag=f"bank{t}"))
+            for lo, hi in PASSES[part]:
+                product(h_banks[t], w_codes, w_scales, t, z_codes, z_scales, slice(lo, hi))
+
+        def copy_h(t, lo, hi, engine="s"):
+            if engine == "s":
+                nc.scalar.copy(h_windows[t][:, lo:hi], h_banks[t][:, lo:hi])
+            else:
+                nc.vector.tensor_copy(h_windows[t][:, lo:hi], h_banks[t][:, lo:hi])
+
+        def square_h(t, lo, hi):
+            nc.scalar.activation(h_sq[t][:, lo:hi], h_windows[t][:, lo:hi], ACT.Square)
+
+        def fetch_partner(t, lo, hi, engine="v"):
+            window = h_windows[t][:].indirect(entries(n3_list, lo, hi))
+            if engine == "s":
+                nc.scalar.activation(partner[t][:, lo:hi], window, ACT.Copy)
+            else:
+                nc.vector.tensor_copy(partner[t][:, lo:hi], window)
+
+        def square_partner(t, lo, hi, engine="s"):
+            if engine == "s":
+                nc.scalar.activation(partner_sq[t][:, lo:hi], partner[t][:, lo:hi], ACT.Square)
+            else:
+                nc.gpsimd.tensor_tensor(partner_sq[t][:, lo:hi], partner[t][:, lo:hi], partner[t][:, lo:hi], ALU.mult)
+
+        def numerator(t, lo, hi):
+            nc.vector.tensor_tensor(numer[t][:, lo:hi], h_banks[t][:, lo:hi], partner[t][:, lo:hi], ALU.mult)
+
+        def invert(t, lo, hi, slot):
+            turned = psum.tile([P, S], F32, name=f"turned{t}_{lo}", tag=f"bank{4 + t}")
+            for c in range(lo, hi, P):
+                nc.tensor.matmul(turned[:, c : c + P], lhsT=h_sq[t][:, c : c + P], rhs=identity[:], is_transpose=True, start=c == lo, stop=False)
+            for c in range(lo, hi, P):
+                nc.tensor.matmul(turned[:, c : c + P], lhsT=partner_sq[t][:, c : c + P], rhs=identity[:], is_transpose=True, start=False, stop=c + P == hi)
+            nc.scalar.activation(root[t][:, lo:hi], turned[:, lo:hi], ACT.Abs_reciprocal_sqrt, bias=half[:])
+
+        def square_root(t, lo, hi):
+            nc.scalar.activation(inverse[t][:, lo:hi], root[t][:, lo:hi], ACT.Square)
+
+        def finish_twice(t, lo, hi, slot):
+            back = psum.tile([P, S], F32, name=f"back{t}_{lo}", tag=f"bank{t}")
+            for c in range(lo, hi, P):
+                nc.tensor.matmul(back[:, c : c + P], lhsT=root[t][:, c : c + P], rhs=identity[:], is_transpose=True, start=True, stop=True)
+            nc.vector.scalar_tensor_tensor(inverse[t][:, lo:hi], numer[t][:, lo:hi], 2.0, back[:, lo:hi], ALU.mult, ALU.mult)
+            nc.vector.tensor_tensor(result[t][:, lo:hi], inverse[t][:, lo:hi], back[:, lo:hi], ALU.mult)
+            nc.sync.dma_start(out_rows[:, t, lo:hi], result[t][:, lo:hi])
+
+        def finish(t, lo, hi, slot):
+            back = psum.tile([P, S], F32, name=f"back{t}_{lo}", tag=f"bank{t}")
+            for c in range(lo, hi, P):
+                nc.tensor.matmul(back[:, c : c + P], lhsT=inverse[t][:, c : c + P], rhs=identity[:], is_transpose=True, start=True, stop=True)
+            nc.vector.scalar_tensor_tensor(result[t][:, lo:hi], numer[t][:, lo:hi], 2.0, back[:, lo:hi], ALU.mult, ALU.mult)
+            nc.sync.dma_start(out_rows[:, t, lo:hi], result[t][:, lo:hi])
+
+
+        (a0, a1), (b0, b1) = PARTS
+        for q in range(4):
+            cast_w(q, "s")
+        quant_w()
+        pieces = [(t, a0, a1) for t in range(PACK)] + [(t, b0, b1) for t in range(PACK)]
+        copy_b(0)
+        for step in range(len(pieces) + 3):
+            if 0 <= step - 3 < len(pieces):
+                gate(*pieces[step - 3])
+            if step - 3 == PACK - 1:
+                weave(a0, a1)
+                quant_z(a0, a1)
+                for t in range(PACK):
+                    product_h(t, 0)
+            if 0 <= step - 2 < len(pieces):
+                tanh(*pieces[step - 2])
+            if 0 <= step - 1 < len(pieces):
+                fetch_b1(*pieces[step - 1])
+            if step < len(pieces):
+                fetch_b2(*pieces[step])
+            if step + 1 < PACK and step + 1 not in (1,):
+                copy_b(step + 1)
+            if step + 1 in (1,):
+                nc.vector.tensor_copy(b_windows[step + 1][:], b_banks[step + 1][:])
+            for t in {7: (0, 1), 8: (2, 3)}.get(step, ()):
+                copy_h(t, a0, a1)
+            for t in {10: (0, 1, 2, 3)}.get(step, ()):
+                square_h(t, a0, a1)
+        weave(b0, b1)
+        quant_z(b0, b1)
+        for t in range(PACK):
+            product_h(t, 1)
+
+        for t in range(PACK):
+            copy_h(t, b0, b1, "v" if t in (0, 1) else "s")
+        items = [(t, 0, 512) for t in range(4)]
+
+        def stage1(n, t, lo, hi):
+            for c in range(lo, hi, 256):
+                fetch_partner(t, c, min(c + 256, hi), "v")
+            if lo == 0:
+                square_h(t, b0, b1)
+
+        def stage2(n, t, lo, hi):
+            square_partner(t, lo, hi, "s")
+
+        def stage3(n, t, lo, hi):
+            invert(t, lo, hi, n % 2)
+
+        def stage4(n, t, lo, hi):
+            if n not in ():
+                square_root(t, lo, hi)
+            numerator(t, lo, hi)
+
+        def stage5(n, t, lo, hi):
+            if n in ():
+                finish_twice(t, lo, hi, n % 2)
+            else:
+                finish(t, lo, hi, n % 2)
+
+        stages = [stage1, stage2, stage3, stage4, stage5]
+        for step in range(len(items) + len(stages) - 1):
+            for depth in range(len(stages)):
+                n = step - depth
+                if 0 <= n < len(items):
+                    stages[depth](n, *items[n])

@@ -44,39 +44,30 @@ def tile_picked_twksjointbharm_none_p_kernel(
         d_word_table = keep.tile([P, G], U32, name="d_word_table", align_bytes=64)
         x_word_table = keep.tile([P, T], U32, name="x_word_table", align_bytes=64)
         key_scales = keep.tile([P, H], U8, name="key_scales", align_bytes=64)
-        w_raw = keep.tile([P, PACK, N], F32, name="w_raw")
+        w_halves = [keep.tile([P, PACK, N // 2], F32, name=f"w_half{u}") for u in range(2)]
         gain = keep.tile([P, PACK], F32, name="gain")
-        nc.gpsimd.memset(d_byte_table[:].bitcast(I32), 0)
-        nc.vector.memset(x_byte_table[:].bitcast(I32), 0)
-        nc.gpsimd.memset(key_scales[:].bitcast(I32), 0)
+        nc.vector.memset(d_byte_table[:].bitcast(I32), 0)
+        nc.gpsimd.memset(x_byte_table[:].bitcast(I32), 0)
+        nc.vector.memset(key_scales[:].bitcast(I32), 0)
         loads = {
             "d": (d_word_table[:].bitcast(I32), d_words[0].rearrange("p n t -> p (n t)").bitcast(I32)),
             "x": (x_word_table[:].bitcast(I32), x_words[0].rearrange("p n t -> p (n t)").bitcast(I32)),
-            "w": (w_raw[:], w1.rearrange("(p j) m -> p j m", j=PACK)),
         }
-
-        def load_x_bytes(q):
-            nc.sync.dma_start(
-                x_byte_table[32 * q : 32 * q + 4, :].bitcast(I32), x_scales[0][4 * q : 4 * q + 4, :].bitcast(I32)
-            )
-
+        nc.scalar.dma_start(gain[:], gn.rearrange("(p t) o -> p (t o)", t=PACK))
         k1_list = load_list("k1_list", k1)
         d_rows = d_scales[0].rearrange("(r s) n -> s r n", s=2)
         for s in range(2):
             nc.sync.dma_start(d_byte_table[s:P:16, :].bitcast(I32), d_rows[s].bitcast(I32))
         two_list = load_list("two_list", two)
         offs_list = load_list("offs_list", offs)
-        load_x_bytes(0)
-        load_x_bytes(1)
         nc.sync.dma_start(*loads["d"])
-        load_x_bytes(2)
-        load_x_bytes(3)
-        n2_list = load_list("n2_list", n2)
-        n1_list = load_list("n1_list", n1)
-        nc.sync.dma_start(*loads["w"])
+        for q in range(4):
+            nc.sync.dma_start(
+                x_byte_table[32 * q : 32 * q + 4, :].bitcast(I32), x_scales[0][4 * q : 4 * q + 4, :].bitcast(I32)
+            )
+        w_rows = w1.rearrange("(p j) m -> p j m", j=PACK)
+        nc.sync.dma_start(w_halves[0][:], w_rows[:, :, : N // 2])
         nc.sync.dma_start(*loads["x"])
-        n3_list = load_list("n3_list", n3)
-        nc.gpsimd.dma_start(gain[:], gn.rearrange("(p t) o -> p (t o)", t=PACK))
 
         gain16 = keep.tile([P, PACK], F32, name="gain16")
         nc.gpsimd.tensor_scalar(gain16[:], gain[:], 0.0625, 0.0, ALU.mult, ALU.add)
@@ -98,7 +89,11 @@ def tile_picked_twksjointbharm_none_p_kernel(
         )
         for r in range(4):
             src = 16 * (r // 2) + r % 2
-            nc.scalar.dma_start(key_scales[r:P:32, :].bitcast(I32), key_bytes_dealt[src:P:32, :].bitcast(I32))
+            nc.sync.dma_start(key_scales[r:P:32, :].bitcast(I32), key_bytes_dealt[src:P:32, :].bitcast(I32))
+        nc.sync.dma_start(w_halves[1][:], w_rows[:, :, N // 2 :])
+        n2_list = load_list("n2_list", n2)
+        n1_list = load_list("n1_list", n1)
+        n3_list = load_list("n3_list", n3)
         key_words = gather("key_words", d_word_table, k1_list, U32)
         key_codes = keep.tile([P, H], U32, name="key_codes", align_bytes=64)
         nc.vector.tensor_copy(
@@ -132,7 +127,7 @@ def tile_picked_twksjointbharm_none_p_kernel(
         z_rows = keep.tile([P, PACK, S], BF16, name="z_rows", align_bytes=64)
         w_grouped = keep.tile([P, N * PACK], BF16, name="w_grouped", align_bytes=64)
         w_out = w_grouped[:].rearrange("p (t m j) -> p m j t", t=PACK, j=PACK)
-        w_in = w_raw[:].rearrange("p j (m t) -> p m j t", t=PACK)
+        w_ins = [w_halves[u][:].rearrange("p j (m t) -> p m j t", t=PACK) for u in range(2)]
         w_codes = keep.tile([P, N], U32, name="w_codes", align_bytes=64)
         w_scales = keep.tile([P, N], U8, name="w_scales", align_bytes=64)
         z_grouped = keep.tile([P, S, PACK], BF16, name="z_grouped", align_bytes=64)
@@ -179,11 +174,7 @@ def tile_picked_twksjointbharm_none_p_kernel(
             )
 
         def cast_w(q, engine, n=4):
-            rows = slice(q * P // n, (q + 1) * P // n)
-            if engine == "s":
-                nc.scalar.copy(w_out[:, rows], w_in[:, rows])
-            else:
-                nc.vector.tensor_copy(w_out[:, rows], w_in[:, rows])
+            nc.scalar.copy(w_out[:, q * P // 2 : (q + 1) * P // 2], w_ins[q])
 
         def quant_w():
             nc.vector.quantize_mx(out=w_codes[:].bitcast(FP8X4), scales=w_scales[:], in_=w_grouped[:])
@@ -260,7 +251,7 @@ def tile_picked_twksjointbharm_none_p_kernel(
 
 
         (a0, a1), (b0, b1) = PARTS
-        for q in range(4):
+        for q in range(2):
             cast_w(q, "s")
         quant_w()
         pieces = [(t, a0, a1) for t in range(PACK)] + [(t, b0, b1) for t in range(PACK)]
@@ -279,9 +270,9 @@ def tile_picked_twksjointbharm_none_p_kernel(
                 fetch_b1(*pieces[step - 1])
             if step < len(pieces):
                 fetch_b2(*pieces[step])
-            if step + 1 < PACK and step + 1 not in (1,):
+            if step + 1 < PACK and step + 1 not in (1, 2):
                 copy_b(step + 1)
-            if step + 1 in (1,):
+            if step + 1 in (1, 2):
                 nc.vector.tensor_copy(b_windows[step + 1][:], b_banks[step + 1][:])
             for t in {7: (0, 1), 8: (2, 3)}.get(step, ()):
                 copy_h(t, a0, a1)

@@ -18,8 +18,15 @@ ALU = mybir.AluOpType
 
 P = 128
 PACK = 4
-PARTS = [(0, 256), (256, 512)]
-PASSES = [[(0, 256)], [(256, 512)]]
+GROUP = 16
+QUADRANT = 32
+X_SCALE_ROW = 4
+ALL = slice(0, S)
+FIRST, SECOND = slice(0, S // 2), slice(S // 2, S)
+LAST = PACK - 1
+B_COPIES_ON_VECTOR = (1, 2)
+FIRST_SQUARES_ON_VECTOR = (2, 3)
+SECOND_COPIES_ON_VECTOR = (0,)
 
 
 def tile_picked_twksjointbharm_none_p_kernel(
@@ -32,12 +39,21 @@ def tile_picked_twksjointbharm_none_p_kernel(
         psum = ctx.enter_context(tc.psum_pool(name="psum", bufs=1))
 
         def load_list(name, src):
-            tile = lists.tile([P, S // 16], U16, name=name)
+            tile = lists.tile([P, S // GROUP], U16, name=name)
             nc.sync.dma_start(tile[:], src)
             return tile
 
-        def tiles(name, dtype=F32):
-            return [keep.tile([P, S], dtype, name=f"{name}{t}") for t in range(PACK)]
+        def entries(list_tile, cols):
+            return list_tile[:, cols.start // GROUP : cols.stop // GROUP]
+
+        def row_tiles(name):
+            return [keep.tile([P, S], F32, name=f"{name}{t}") for t in range(PACK)]
+
+        def bank(name, number):
+            return psum.tile([P, S], F32, name=name, tag=f"bank{number}")
+
+        def words_of(table):
+            return table[0].rearrange("p n t -> p (n t)").bitcast(I32)
 
         d_byte_table = keep.tile([P, G], U8, name="d_byte_table", align_bytes=64)
         x_byte_table = keep.tile([P, T], U8, name="x_byte_table", align_bytes=64)
@@ -49,66 +65,64 @@ def tile_picked_twksjointbharm_none_p_kernel(
         nc.vector.memset(d_byte_table[:].bitcast(I32), 0)
         nc.gpsimd.memset(x_byte_table[:].bitcast(I32), 0)
         nc.vector.memset(key_scales[:].bitcast(I32), 0)
-        loads = {
-            "d": (d_word_table[:].bitcast(I32), d_words[0].rearrange("p n t -> p (n t)").bitcast(I32)),
-            "x": (x_word_table[:].bitcast(I32), x_words[0].rearrange("p n t -> p (n t)").bitcast(I32)),
-        }
+
         nc.scalar.dma_start(gain[:], gn.rearrange("(p t) o -> p (t o)", t=PACK))
         k1_list = load_list("k1_list", k1)
         d_rows = d_scales[0].rearrange("(r s) n -> s r n", s=2)
         for s in range(2):
-            nc.sync.dma_start(d_byte_table[s:P:16, :].bitcast(I32), d_rows[s].bitcast(I32))
+            nc.sync.dma_start(d_byte_table[s:P:GROUP, :].bitcast(I32), d_rows[s].bitcast(I32))
         two_list = load_list("two_list", two)
         offs_list = load_list("offs_list", offs)
-        nc.sync.dma_start(*loads["d"])
-        for q in range(4):
-            nc.sync.dma_start(
-                x_byte_table[32 * q : 32 * q + 4, :].bitcast(I32), x_scales[0][4 * q : 4 * q + 4, :].bitcast(I32)
-            )
+        nc.sync.dma_start(d_word_table[:].bitcast(I32), words_of(d_words))
+        x_rows = x_scales[0].rearrange("(q r) n -> r q n", r=4)
+        for r in range(4):
+            nc.sync.dma_start(x_byte_table[X_SCALE_ROW + r : P : QUADRANT, :].bitcast(I32), x_rows[r].bitcast(I32))
         w_rows = w1.rearrange("(p j) m -> p j m", j=PACK)
         nc.sync.dma_start(w_halves[0][:], w_rows[:, :, : N // 2])
-        nc.sync.dma_start(*loads["x"])
+        nc.sync.dma_start(x_word_table[:].bitcast(I32), words_of(x_words))
+        nc.sync.dma_start(w_halves[1][:], w_rows[:, :, N // 2 :])
 
         gain16 = keep.tile([P, PACK], F32, name="gain16")
         nc.gpsimd.tensor_scalar(gain16[:], gain[:], 0.0625, 0.0, ALU.mult, ALU.add)
         identity = keep.tile([P, P], F32, name="identity")
         make_identity(nc, identity[:])
-        half = keep.tile([P, 1], F32, name="half")
-        nc.gpsimd.memset(half[:], 0.5)
+        point_five = keep.tile([P, 1], F32, name="point_five")
+        nc.gpsimd.memset(point_five[:], 0.5)
 
-        def gather(name, table, offsets, dtype):
+        def gather_packed(name, table, list_tile, dtype):
             tile = keep.tile([P, S], dtype, name=name, align_bytes=64)
-            nc.vector.tensor_copy(tile[:], table[:].indirect(offsets[:]))
+            nc.vector.tensor_copy(tile[:], table[:].indirect(list_tile[:]))
             return tile
 
-        key_bytes = gather("key_bytes", d_byte_table, k1_list, U8)
+        key_bytes = gather_packed("key_bytes", d_byte_table, k1_list, U8)
         key_bytes_dealt = keep.tile([P, H], U8, name="key_bytes_dealt", align_bytes=64)
         nc.vector.tensor_copy(
             key_bytes_dealt[:].rearrange("p (t m) -> p t m", t=PACK),
             key_bytes[:].rearrange("p (m t) -> p t m", t=PACK),
         )
         for r in range(4):
-            src = 16 * (r // 2) + r % 2
-            nc.sync.dma_start(key_scales[r:P:32, :].bitcast(I32), key_bytes_dealt[src:P:32, :].bitcast(I32))
-        nc.sync.dma_start(w_halves[1][:], w_rows[:, :, N // 2 :])
+            source = GROUP * (r // 2) + r % 2
+            nc.sync.dma_start(
+                key_scales[r:P:QUADRANT, :].bitcast(I32), key_bytes_dealt[source:P:QUADRANT, :].bitcast(I32)
+            )
         n2_list = load_list("n2_list", n2)
         n1_list = load_list("n1_list", n1)
         n3_list = load_list("n3_list", n3)
-        key_words = gather("key_words", d_word_table, k1_list, U32)
+        key_words = gather_packed("key_words", d_word_table, k1_list, U32)
         key_codes = keep.tile([P, H], U32, name="key_codes", align_bytes=64)
         nc.vector.tensor_copy(
             key_codes[:].rearrange("p (t m) -> p m t", t=PACK),
             key_words[:].rearrange("p (m t) -> p m t", t=PACK),
         )
-        b_scales = gather("b_scales", x_byte_table, two_list, U8)
-        a_scales = gather("a_scales", x_byte_table, offs_list, U8)
-        b_codes = gather("b_codes", x_word_table, two_list, U32)
-        a_codes = gather("a_codes", x_word_table, offs_list, U32)
+        b_scales = gather_packed("b_scales", x_byte_table, two_list, U8)
+        a_scales = gather_packed("a_scales", x_byte_table, offs_list, U8)
+        b_codes = gather_packed("b_codes", x_word_table, two_list, U32)
+        a_codes = gather_packed("a_codes", x_word_table, offs_list, U32)
 
-        def product(bank, lhs_codes, lhs_scales, t, rhs_codes, rhs_scales, cols):
+        def product(result_bank, t, lhs_codes, lhs_scales, rhs_codes, rhs_scales, cols):
             rows = slice(t * P, (t + 1) * P)
             nc.tensor.matmul_mx(
-                out=bank[:, cols],
+                out=result_bank[:, cols],
                 lhsT=lhs_codes[:, rows].bitcast(FP8X4),
                 lhsT_scale=lhs_scales[:, rows],
                 rhs=rhs_codes[:, cols].bitcast(FP8X4),
@@ -117,202 +131,161 @@ def tile_picked_twksjointbharm_none_p_kernel(
                 stop=True,
             )
 
-        b_banks = [psum.tile([P, S], F32, name=f"b{t}", tag=f"bank{t}") for t in range(PACK)]
-        a_banks = [psum.tile([P, S], F32, name=f"a{t}", tag=f"bank{4 + t}") for t in range(PACK)]
+        b_banks = [bank(f"b{t}", t) for t in range(PACK)]
+        a_banks = [bank(f"a{t}", PACK + t) for t in range(PACK)]
         for t in range(PACK):
-            product(b_banks[t], key_codes, key_scales, t, b_codes, b_scales, slice(0, S))
+            product(b_banks[t], t, key_codes, key_scales, b_codes, b_scales[X_SCALE_ROW:, :], ALL)
         for t in range(PACK):
-            product(a_banks[t], key_codes, key_scales, t, a_codes, a_scales, slice(0, S))
+            product(a_banks[t], t, key_codes, key_scales, a_codes, a_scales[X_SCALE_ROW:, :], ALL)
 
         z_rows = keep.tile([P, PACK, S], BF16, name="z_rows", align_bytes=64)
         w_grouped = keep.tile([P, N * PACK], BF16, name="w_grouped", align_bytes=64)
-        w_out = w_grouped[:].rearrange("p (t m j) -> p m j t", t=PACK, j=PACK)
-        w_ins = [w_halves[u][:].rearrange("p j (m t) -> p m j t", t=PACK) for u in range(2)]
         w_codes = keep.tile([P, N], U32, name="w_codes", align_bytes=64)
         w_scales = keep.tile([P, N], U8, name="w_scales", align_bytes=64)
         z_grouped = keep.tile([P, S, PACK], BF16, name="z_grouped", align_bytes=64)
         z_codes = keep.tile([P, S], U32, name="z_codes", align_bytes=64)
         z_scales = keep.tile([P, S], U8, name="z_scales", align_bytes=64)
-        b_windows = tiles("b_window")
-        minus_b2 = tiles("minus_b2_")
-        diff = tiles("diff")
-        squash = tiles("squash")
-        h_windows = tiles("h_window")
-        partner = tiles("partner")
-        h_sq = tiles("h_sq")
-        partner_sq = tiles("partner_sq")
-        denom = tiles("denom")
-        root = tiles("root")
-        inverse = tiles("inverse")
-        numer = tiles("numer")
-        result = tiles("result")
-        out_rows = out.rearrange("(p t) j -> p t j", t=PACK)
-        h_banks = []
+        b_windows = row_tiles("b_window")
+        minus_b2 = row_tiles("minus_b2_")
+        diff = row_tiles("diff")
+        squash = row_tiles("squash")
+        h_windows = row_tiles("h_window")
+        partner = row_tiles("partner")
+        h_sq = row_tiles("h_sq")
+        partner_sq = row_tiles("partner_sq")
+        root = row_tiles("root")
+        inverse = row_tiles("inverse")
+        numer = row_tiles("numer")
+        result = row_tiles("result")
 
-        def entries(offsets, lo, hi):
-            return offsets[:, lo // 16 : hi // 16]
-
-        def copy_b(t):
-            nc.scalar.copy(b_windows[t][:], b_banks[t][:])
-
-        def fetch_b2(t, lo, hi):
-            nc.scalar.activation(
-                minus_b2[t][:, lo:hi], b_windows[t][:].indirect(entries(n2_list, lo, hi)), ACT.Copy, scale=-1.0
+        w_dealt = w_grouped[:].rearrange("p (t m j) -> p m j t", t=PACK, j=PACK)
+        for u in range(2):
+            nc.scalar.copy(
+                w_dealt[:, u * P // 2 : (u + 1) * P // 2], w_halves[u][:].rearrange("p j (m t) -> p m j t", t=PACK)
             )
+        nc.vector.quantize_mx(out=w_codes[:].bitcast(FP8X4), scales=w_scales[:], in_=w_grouped[:])
 
-        def fetch_b1(t, lo, hi):
-            nc.vector.tensor_tensor(
-                diff[t][:, lo:hi], b_windows[t][:].indirect(entries(n1_list, lo, hi)), minus_b2[t][:, lo:hi], ALU.add
-            )
+        def copy_out(on_vector, target, source):
+            if on_vector:
+                nc.vector.tensor_copy(target, source)
+            else:
+                nc.scalar.copy(target, source)
 
-        def tanh(t, lo, hi):
-            nc.scalar.activation(squash[t][:, lo:hi], diff[t][:, lo:hi], ACT.Tanh, scale=0.0625)
+        def fetch_b2(t, cols):
+            window = b_windows[t][:].indirect(entries(n2_list, cols))
+            nc.scalar.activation(minus_b2[t][:, cols], window, ACT.Copy, scale=-1.0)
 
-        def gate(t, lo, hi):
+        def fetch_b1(t, cols):
+            window = b_windows[t][:].indirect(entries(n1_list, cols))
+            nc.vector.tensor_tensor(diff[t][:, cols], window, minus_b2[t][:, cols], ALU.add)
+
+        def tanh(t, cols):
+            nc.scalar.activation(squash[t][:, cols], diff[t][:, cols], ACT.Tanh, scale=0.0625)
+
+        def gate(t, cols):
             nc.vector.scalar_tensor_tensor(
-                z_rows[:, t, lo:hi], a_banks[t][:, lo:hi], gain16[:, t : t + 1], squash[t][:, lo:hi], ALU.mult, ALU.mult
+                z_rows[:, t, cols], a_banks[t][:, cols], gain16[:, t : t + 1], squash[t][:, cols], ALU.mult, ALU.mult
             )
 
-        def cast_w(q, engine, n=4):
-            nc.scalar.copy(w_out[:, q * P // 2 : (q + 1) * P // 2], w_ins[q])
-
-        def quant_w():
-            nc.vector.quantize_mx(out=w_codes[:].bitcast(FP8X4), scales=w_scales[:], in_=w_grouped[:])
-
-        def weave(lo, hi):
+        def quantize_z(cols):
             nc.vector.tensor_copy(
-                z_grouped[:, lo:hi, :].rearrange("p (c i) t -> p c t i", i=4),
-                z_rows[:, :, lo:hi].rearrange("p t (c i) -> p c t i", i=4),
+                z_grouped[:, cols, :].rearrange("p (c i) t -> p c t i", i=4),
+                z_rows[:, :, cols].rearrange("p t (c i) -> p c t i", i=4),
             )
-
-        def quant_z(lo, hi):
             nc.vector.quantize_mx(
-                out=z_codes[:, lo:hi].bitcast(FP8X4),
-                scales=z_scales[:, lo:hi],
-                in_=z_grouped[:, lo:hi, :].rearrange("p j t -> p (j t)"),
+                out=z_codes[:, cols].bitcast(FP8X4),
+                scales=z_scales[:, cols],
+                in_=z_grouped[:, cols, :].rearrange("p j t -> p (j t)"),
             )
 
-        def product_h(t, part):
-            if part == 0:
-                h_banks.append(psum.tile([P, S], F32, name=f"h{t}", tag=f"bank{t}"))
-            for lo, hi in PASSES[part]:
-                product(h_banks[t], w_codes, w_scales, t, z_codes, z_scales, slice(lo, hi))
+        def square_h(t, cols):
+            nc.scalar.activation(h_sq[t][:, cols], h_windows[t][:, cols], ACT.Square)
 
-        def copy_h(t, lo, hi, engine="s"):
-            if engine == "s":
-                nc.scalar.copy(h_windows[t][:, lo:hi], h_banks[t][:, lo:hi])
-            else:
-                nc.vector.tensor_copy(h_windows[t][:, lo:hi], h_banks[t][:, lo:hi])
-
-        def square_h(t, lo, hi):
-            nc.scalar.activation(h_sq[t][:, lo:hi], h_windows[t][:, lo:hi], ACT.Square)
-
-        def fetch_partner(t, lo, hi, engine="v"):
-            window = h_windows[t][:].indirect(entries(n3_list, lo, hi))
-            if engine == "s":
-                nc.scalar.activation(partner[t][:, lo:hi], window, ACT.Copy)
-            else:
-                nc.vector.tensor_copy(partner[t][:, lo:hi], window)
-
-        def square_partner(t, lo, hi, engine="s"):
-            if engine == "s":
-                nc.scalar.activation(partner_sq[t][:, lo:hi], partner[t][:, lo:hi], ACT.Square)
-            else:
-                nc.gpsimd.tensor_tensor(partner_sq[t][:, lo:hi], partner[t][:, lo:hi], partner[t][:, lo:hi], ALU.mult)
-
-        def numerator(t, lo, hi):
-            nc.vector.tensor_tensor(numer[t][:, lo:hi], h_banks[t][:, lo:hi], partner[t][:, lo:hi], ALU.mult)
-
-        def invert(t, lo, hi, slot):
-            turned = psum.tile([P, S], F32, name=f"turned{t}_{lo}", tag=f"bank{4 + t}")
-            for c in range(lo, hi, P):
-                nc.tensor.matmul(turned[:, c : c + P], lhsT=h_sq[t][:, c : c + P], rhs=identity[:], is_transpose=True, start=c == lo, stop=False)
-            for c in range(lo, hi, P):
-                nc.tensor.matmul(turned[:, c : c + P], lhsT=partner_sq[t][:, c : c + P], rhs=identity[:], is_transpose=True, start=False, stop=c + P == hi)
-            nc.scalar.activation(root[t][:, lo:hi], turned[:, lo:hi], ACT.Abs_reciprocal_sqrt, bias=half[:])
-
-        def square_root(t, lo, hi):
-            nc.scalar.activation(inverse[t][:, lo:hi], root[t][:, lo:hi], ACT.Square)
-
-        def finish_twice(t, lo, hi, slot):
-            back = psum.tile([P, S], F32, name=f"back{t}_{lo}", tag=f"bank{t}")
-            for c in range(lo, hi, P):
-                nc.tensor.matmul(back[:, c : c + P], lhsT=root[t][:, c : c + P], rhs=identity[:], is_transpose=True, start=True, stop=True)
-            nc.vector.scalar_tensor_tensor(inverse[t][:, lo:hi], numer[t][:, lo:hi], 2.0, back[:, lo:hi], ALU.mult, ALU.mult)
-            nc.vector.tensor_tensor(result[t][:, lo:hi], inverse[t][:, lo:hi], back[:, lo:hi], ALU.mult)
-            nc.sync.dma_start(out_rows[:, t, lo:hi], result[t][:, lo:hi])
-
-        def finish(t, lo, hi, slot):
-            back = psum.tile([P, S], F32, name=f"back{t}_{lo}", tag=f"bank{t}")
-            for c in range(lo, hi, P):
-                nc.tensor.matmul(back[:, c : c + P], lhsT=inverse[t][:, c : c + P], rhs=identity[:], is_transpose=True, start=True, stop=True)
-            nc.vector.scalar_tensor_tensor(result[t][:, lo:hi], numer[t][:, lo:hi], 2.0, back[:, lo:hi], ALU.mult, ALU.mult)
-            nc.sync.dma_start(out_rows[:, t, lo:hi], result[t][:, lo:hi])
-
-
-        (a0, a1), (b0, b1) = PARTS
-        for q in range(2):
-            cast_w(q, "s")
-        quant_w()
-        pieces = [(t, a0, a1) for t in range(PACK)] + [(t, b0, b1) for t in range(PACK)]
-        copy_b(0)
-        for step in range(len(pieces) + 3):
-            if 0 <= step - 3 < len(pieces):
-                gate(*pieces[step - 3])
-            if step - 3 == PACK - 1:
-                weave(a0, a1)
-                quant_z(a0, a1)
-                for t in range(PACK):
-                    product_h(t, 0)
-            if 0 <= step - 2 < len(pieces):
-                tanh(*pieces[step - 2])
-            if 0 <= step - 1 < len(pieces):
-                fetch_b1(*pieces[step - 1])
-            if step < len(pieces):
-                fetch_b2(*pieces[step])
-            if step + 1 < PACK and step + 1 not in (1, 2):
-                copy_b(step + 1)
-            if step + 1 in (1, 2):
-                nc.vector.tensor_copy(b_windows[step + 1][:], b_banks[step + 1][:])
-            for t in {7: (0, 1), 8: (2, 3)}.get(step, ()):
-                copy_h(t, a0, a1)
-            for t in {10: (0, 1, 2, 3)}.get(step, ()):
-                square_h(t, a0, a1)
-        weave(b0, b1)
-        quant_z(b0, b1)
+        pieces = [(t, cols) for cols in (FIRST, SECOND) for t in range(PACK)]
+        stages = (fetch_b2, fetch_b1, tanh, gate)
+        first_gated = LAST + len(stages) - 1
+        h_banks = []
+        nc.scalar.copy(b_windows[0][:], b_banks[0][:])
+        for step in range(len(pieces) + len(stages) - 1):
+            for lag in reversed(range(len(stages))):
+                if 0 <= step - lag < len(pieces):
+                    stages[lag](*pieces[step - lag])
+                if step == first_gated and stages[lag] is gate:
+                    quantize_z(FIRST)
+                    for t in range(PACK):
+                        h_banks.append(bank(f"h{t}", t))
+                        product(h_banks[t], t, w_codes, w_scales, z_codes, z_scales, FIRST)
+            if step + 1 < PACK:
+                copy_out(step + 1 in B_COPIES_ON_VECTOR, b_windows[step + 1][:], b_banks[step + 1][:])
+            if 1 <= step - first_gated <= 2:
+                for t in (2 * (step - first_gated) - 2, 2 * (step - first_gated) - 1):
+                    nc.scalar.copy(h_windows[t][:, FIRST], h_banks[t][:, FIRST])
         for t in range(PACK):
-            product_h(t, 1)
-
+            if t not in FIRST_SQUARES_ON_VECTOR:
+                square_h(t, FIRST)
+        quantize_z(SECOND)
+        for t in FIRST_SQUARES_ON_VECTOR:
+            nc.vector.tensor_tensor(h_sq[t][:, FIRST], h_banks[t][:, FIRST], h_windows[t][:, FIRST], ALU.mult)
         for t in range(PACK):
-            copy_h(t, b0, b1, "v" if t in (0, 1) else "s")
-        items = [(t, 0, 512) for t in range(4)]
+            product(h_banks[t], t, w_codes, w_scales, z_codes, z_scales, SECOND)
+        for t in range(PACK):
+            copy_out(t in SECOND_COPIES_ON_VECTOR, h_windows[t][:, SECOND], h_banks[t][:, SECOND])
 
-        def stage1(n, t, lo, hi):
-            for c in range(lo, hi, 256):
-                fetch_partner(t, c, min(c + 256, hi), "v")
-            if lo == 0:
-                square_h(t, b0, b1)
+        out_rows = out.rearrange("(p t) j -> p t j", t=PACK)
 
-        def stage2(n, t, lo, hi):
-            square_partner(t, lo, hi, "s")
+        def turn(target_bank, sources, cols):
+            blocks = [(source, c) for source in sources for c in range(cols.start, cols.stop, P)]
+            for n, (source, c) in enumerate(blocks):
+                nc.tensor.matmul(
+                    target_bank[:, c : c + P],
+                    lhsT=source[:, c : c + P],
+                    rhs=identity[:],
+                    is_transpose=True,
+                    start=n == 0 or len(sources) == 1,
+                    stop=n == len(blocks) - 1 or len(sources) == 1,
+                )
 
-        def stage3(n, t, lo, hi):
-            invert(t, lo, hi, n % 2)
+        def fetch_partner(t):
+            for cols in (FIRST, SECOND):
+                nc.vector.tensor_copy(partner[t][:, cols], h_windows[t][:].indirect(entries(n3_list, cols)))
+            square_h(t, SECOND)
 
-        def stage4(n, t, lo, hi):
-            if n not in ():
-                square_root(t, lo, hi)
-            numerator(t, lo, hi)
+        def square_partner(t):
+            nc.scalar.activation(partner_sq[t][:], partner[t][:], ACT.Square)
 
-        def stage5(n, t, lo, hi):
-            if n in ():
-                finish_twice(t, lo, hi, n % 2)
-            else:
-                finish(t, lo, hi, n % 2)
+        def inverse_root(t):
+            turned = bank(f"turned{t}", PACK + t)
+            turn(turned, (h_sq[t], partner_sq[t]), ALL)
+            nc.scalar.activation(root[t][:], turned[:], ACT.Abs_reciprocal_sqrt, bias=point_five[:])
 
-        stages = [stage1, stage2, stage3, stage4, stage5]
-        for step in range(len(items) + len(stages) - 1):
-            for depth in range(len(stages)):
-                n = step - depth
-                if 0 <= n < len(items):
-                    stages[depth](n, *items[n])
+        def square_root(t, cols):
+            nc.scalar.activation(inverse[t][:, cols], root[t][:, cols], ACT.Square)
+
+        def finish(t, cols, number):
+            back = bank(f"back{t}_{cols.start}", number)
+            turn(back, (inverse[t],), cols)
+            nc.vector.scalar_tensor_tensor(
+                result[t][:, cols], numer[t][:, cols], 2.0, back[:, cols], ALU.mult, ALU.mult
+            )
+            nc.sync.dma_start(out_rows[:, t, cols], result[t][:, cols])
+
+        for step in range(PACK + 3):
+            if step < PACK:
+                fetch_partner(step)
+            if 0 <= step - 1 < PACK:
+                square_partner(step - 1)
+            if step - 2 == LAST:
+                square_root(LAST - 1, ALL)
+            if 0 <= step - 2 < PACK:
+                inverse_root(step - 2)
+            t = step - 3
+            if t >= 0:
+                nc.vector.tensor_tensor(numer[t][:], h_banks[t][:], partner[t][:], ALU.mult)
+            if 0 <= t < LAST:
+                if t != LAST - 1:
+                    square_root(t, ALL)
+                finish(t, ALL, t)
+            if t == LAST:
+                for cols, number in ((FIRST, LAST), (SECOND, 0)):
+                    square_root(t, cols)
+                    finish(t, cols, number)

@@ -157,6 +157,7 @@ def tile_picked_twksjointbharm_none_p_kernel(
         inverse = row_tiles("inverse")
         numer = row_tiles("numer")
         result = row_tiles("result")
+        unread = keep.tile([P, 1], F32, name="unread")
 
         w_dealt = w_grouped[:].rearrange("p (t m j) -> p m j t", t=PACK, j=PACK)
         for u in range(2):
@@ -223,6 +224,9 @@ def tile_picked_twksjointbharm_none_p_kernel(
         for t in range(PACK):
             if t not in FIRST_SQUARES_ON_VECTOR:
                 square_h(t, FIRST)
+        nc.scalar.activation(
+            unread[:], squash[LAST][:, S - 1 : S], ACT.Abs_reciprocal_sqrt, bias=point_five[:], scale=0.25
+        )
         quantize_z(SECOND)
         for t in FIRST_SQUARES_ON_VECTOR:
             nc.vector.tensor_tensor(h_sq[t][:, FIRST], h_banks[t][:, FIRST], h_windows[t][:, FIRST], ALU.mult)

@@ -21,12 +21,13 @@ PACK = 4
 GROUP = 16
 QUADRANT = 32
 X_SCALE_ROW = 4
+D_SCALE_STEP = 8
 ALL = slice(0, S)
 FIRST, SECOND = slice(0, S // 2), slice(S // 2, S)
 LAST = PACK - 1
 B_COPIES_ON_VECTOR = (1, 2)
 FIRST_SQUARES_ON_VECTOR = (2, 3)
-SECOND_COPIES_ON_VECTOR = (0,)
+TANH_LAG, GATE_LAG = 4, 5
 
 
 def tile_picked_twksjointbharm_none_p_kernel(
@@ -63,27 +64,28 @@ def tile_picked_twksjointbharm_none_p_kernel(
         w_halves = [keep.tile([P, PACK, N // 2], F32, name=f"w_half{u}") for u in range(2)]
         gain = keep.tile([P, PACK], F32, name="gain")
         nc.vector.memset(d_byte_table[:].bitcast(I32), 0)
-        nc.gpsimd.memset(x_byte_table[:].bitcast(I32), 0)
+        nc.vector.memset(x_byte_table[:].bitcast(I32), 0)
         nc.vector.memset(key_scales[:].bitcast(I32), 0)
 
         nc.scalar.dma_start(gain[:], gn.rearrange("(p t) o -> p (t o)", t=PACK))
         k1_list = load_list("k1_list", k1)
-        d_rows = d_scales[0].rearrange("(r s) n -> s r n", s=2)
-        for s in range(2):
-            nc.sync.dma_start(d_byte_table[s:P:GROUP, :].bitcast(I32), d_rows[s].bitcast(I32))
+        nc.sync.dma_start(d_byte_table[0:P:D_SCALE_STEP, :].bitcast(I32), d_scales[0].bitcast(I32))
         two_list = load_list("two_list", two)
         offs_list = load_list("offs_list", offs)
         nc.sync.dma_start(d_word_table[:].bitcast(I32), words_of(d_words))
         x_rows = x_scales[0].rearrange("(q r) n -> r q n", r=4)
         for r in range(4):
             nc.sync.dma_start(x_byte_table[X_SCALE_ROW + r : P : QUADRANT, :].bitcast(I32), x_rows[r].bitcast(I32))
+        n2_list = load_list("n2_list", n2)
         w_rows = w1.rearrange("(p j) m -> p j m", j=PACK)
         nc.sync.dma_start(w_halves[0][:], w_rows[:, :, : N // 2])
         nc.sync.dma_start(x_word_table[:].bitcast(I32), words_of(x_words))
         nc.sync.dma_start(w_halves[1][:], w_rows[:, :, N // 2 :])
+        n1_list = load_list("n1_list", n1)
+        n3_list = load_list("n3_list", n3)
 
         gain16 = keep.tile([P, PACK], F32, name="gain16")
-        nc.gpsimd.tensor_scalar(gain16[:], gain[:], 0.0625, 0.0, ALU.mult, ALU.add)
+        nc.scalar.activation(gain16[:], gain[:], ACT.Copy, scale=0.0625)
         identity = keep.tile([P, P], F32, name="identity")
         make_identity(nc, identity[:])
         point_five = keep.tile([P, 1], F32, name="point_five")
@@ -101,13 +103,10 @@ def tile_picked_twksjointbharm_none_p_kernel(
             key_bytes[:].rearrange("p (m t) -> p t m", t=PACK),
         )
         for r in range(4):
-            source = GROUP * (r // 2) + r % 2
+            source = D_SCALE_STEP * r
             nc.sync.dma_start(
                 key_scales[r:P:QUADRANT, :].bitcast(I32), key_bytes_dealt[source:P:QUADRANT, :].bitcast(I32)
             )
-        n2_list = load_list("n2_list", n2)
-        n1_list = load_list("n1_list", n1)
-        n3_list = load_list("n3_list", n3)
         key_words = gather_packed("key_words", d_word_table, k1_list, U32)
         key_codes = keep.tile([P, H], U32, name="key_codes", align_bytes=64)
         nc.vector.tensor_copy(
@@ -166,11 +165,11 @@ def tile_picked_twksjointbharm_none_p_kernel(
             )
         nc.vector.quantize_mx(out=w_codes[:].bitcast(FP8X4), scales=w_scales[:], in_=w_grouped[:])
 
-        def copy_out(on_vector, target, source):
-            if on_vector:
-                nc.vector.tensor_copy(target, source)
+        def copy_b(t):
+            if t in B_COPIES_ON_VECTOR:
+                nc.vector.tensor_copy(b_windows[t][:], b_banks[t][:])
             else:
-                nc.scalar.copy(target, source)
+                nc.scalar.copy(b_windows[t][:], b_banks[t][:])
 
         def fetch_b2(t, cols):
             window = b_windows[t][:].indirect(entries(n2_list, cols))
@@ -203,21 +202,21 @@ def tile_picked_twksjointbharm_none_p_kernel(
             nc.scalar.activation(h_sq[t][:, cols], h_windows[t][:, cols], ACT.Square)
 
         pieces = [(t, cols) for cols in (FIRST, SECOND) for t in range(PACK)]
-        stages = (fetch_b2, fetch_b1, tanh, gate)
-        first_gated = LAST + len(stages) - 1
+        stages = ((gate, GATE_LAG), (tanh, TANH_LAG), (fetch_b1, 1), (fetch_b2, 0))
+        first_gated = LAST + GATE_LAG
         h_banks = []
-        nc.scalar.copy(b_windows[0][:], b_banks[0][:])
-        for step in range(len(pieces) + len(stages) - 1):
-            for lag in reversed(range(len(stages))):
+        copy_b(0)
+        for step in range(len(pieces) + GATE_LAG):
+            for stage, lag in stages:
                 if 0 <= step - lag < len(pieces):
-                    stages[lag](*pieces[step - lag])
-                if step == first_gated and stages[lag] is gate:
+                    stage(*pieces[step - lag])
+                if step == first_gated and stage is gate:
                     quantize_z(FIRST)
                     for t in range(PACK):
                         h_banks.append(bank(f"h{t}", t))
                         product(h_banks[t], t, w_codes, w_scales, z_codes, z_scales, FIRST)
             if step + 1 < PACK:
-                copy_out(step + 1 in B_COPIES_ON_VECTOR, b_windows[step + 1][:], b_banks[step + 1][:])
+                copy_b(step + 1)
             if 1 <= step - first_gated <= 2:
                 for t in (2 * (step - first_gated) - 2, 2 * (step - first_gated) - 1):
                     nc.scalar.copy(h_windows[t][:, FIRST], h_banks[t][:, FIRST])
@@ -229,11 +228,11 @@ def tile_picked_twksjointbharm_none_p_kernel(
         )
         quantize_z(SECOND)
         for t in FIRST_SQUARES_ON_VECTOR:
-            nc.vector.tensor_tensor(h_sq[t][:, FIRST], h_banks[t][:, FIRST], h_windows[t][:, FIRST], ALU.mult)
+            nc.vector.tensor_tensor(h_sq[t][:, FIRST], h_windows[t][:, FIRST], h_windows[t][:, FIRST], ALU.mult)
         for t in range(PACK):
             product(h_banks[t], t, w_codes, w_scales, z_codes, z_scales, SECOND)
         for t in range(PACK):
-            copy_out(t in SECOND_COPIES_ON_VECTOR, h_windows[t][:, SECOND], h_banks[t][:, SECOND])
+            nc.scalar.copy(h_windows[t][:, SECOND], h_banks[t][:, SECOND])
 
         out_rows = out.rearrange("(p t) j -> p t j", t=PACK)
 

from contextlib import ExitStack

import concourse.mybir as mybir
from concourse.masks import make_identity

K, T, S, N, G, H = 512, 2048, 512, 512, 2048, 512
FLOPS = 2 * K * H * S * 2 + 2 * H * N * S

F32 = mybir.dt.float32
BF16 = mybir.dt.bfloat16
I32 = mybir.dt.int32
U32 = mybir.dt.uint32
U16 = mybir.dt.uint16
U8 = mybir.dt.uint8
FP8X4 = mybir.dt.float8_e4m3fn_x4
ACT = mybir.ActivationFunctionType
ALU = mybir.AluOpType

P = 128
PACK = 4
GROUP = 16
QUADRANT = 32
X_SCALE_ROW = 4
D_SCALE_STEP = 8
ALL = slice(0, S)
FIRST, SECOND = slice(0, S // 2), slice(S // 2, S)
LAST = PACK - 1
B_COPIES_ON_VECTOR = (1, 2)
FIRST_SQUARES_ON_VECTOR = (2, 3)
TANH_LAG, GATE_LAG = 4, 5


def tile_picked_twksjointbharm_none_p_kernel(
    tc, x_words, x_scales, d_words, d_scales, gn, w1, offs, k1, two, n1, n2, n3, out
):
    nc = tc.nc
    with ExitStack() as ctx:
        lists = ctx.enter_context(tc.tile_pool(name="lists", bufs=1))
        keep = ctx.enter_context(tc.tile_pool(name="keep", bufs=1))
        psum = ctx.enter_context(tc.psum_pool(name="psum", bufs=1))

        def load_list(name, src):
            tile = lists.tile([P, S // GROUP], U16, name=name)
            nc.sync.dma_start(tile[:], src)
            return tile

        def entries(list_tile, cols):
            return list_tile[:, cols.start // GROUP : cols.stop // GROUP]

        def row_tiles(name):
            return [keep.tile([P, S], F32, name=f"{name}{t}") for t in range(PACK)]

        def bank(name, number):
            return psum.tile([P, S], F32, name=name, tag=f"bank{number}")

        def words_of(table):
            return table[0].rearrange("p n t -> p (n t)").bitcast(I32)

        d_byte_table = keep.tile([P, G], U8, name="d_byte_table", align_bytes=64)
        x_byte_table = keep.tile([P, T], U8, name="x_byte_table", align_bytes=64)
        d_word_table = keep.tile([P, G], U32, name="d_word_table", align_bytes=64)
        x_word_table = keep.tile([P, T], U32, name="x_word_table", align_bytes=64)
        key_scales = keep.tile([P, H], U8, name="key_scales", align_bytes=64)
        w_halves = [keep.tile([P, PACK, N // 2], F32, name=f"w_half{u}") for u in range(2)]
        gain = keep.tile([P, PACK], F32, name="gain")
        nc.vector.memset(d_byte_table[:].bitcast(I32), 0)
        nc.vector.memset(x_byte_table[:].bitcast(I32), 0)
        nc.vector.memset(key_scales[:].bitcast(I32), 0)

        nc.scalar.dma_start(gain[:], gn.rearrange("(p t) o -> p (t o)", t=PACK))
        k1_list = load_list("k1_list", k1)
        nc.sync.dma_start(d_byte_table[0:P:D_SCALE_STEP, :].bitcast(I32), d_scales[0].bitcast(I32))
        two_list = load_list("two_list", two)
        offs_list = load_list("offs_list", offs)
        nc.sync.dma_start(d_word_table[:].bitcast(I32), words_of(d_words))
        x_rows = x_scales[0].rearrange("(q r) n -> r q n", r=4)
        for r in range(4):
            nc.sync.dma_start(x_byte_table[X_SCALE_ROW + r : P : QUADRANT, :].bitcast(I32), x_rows[r].bitcast(I32))
        n2_list = load_list("n2_list", n2)
        w_rows = w1.rearrange("(p j) m -> p j m", j=PACK)
        nc.sync.dma_start(w_halves[0][:], w_rows[:, :, : N // 2])
        nc.sync.dma_start(x_word_table[:].bitcast(I32), words_of(x_words))
        nc.sync.dma_start(w_halves[1][:], w_rows[:, :, N // 2 :])
        n1_list = load_list("n1_list", n1)
        n3_list = load_list("n3_list", n3)

        gain16 = keep.tile([P, PACK], F32, name="gain16")
        nc.scalar.activation(gain16[:], gain[:], ACT.Copy, scale=0.0625)
        identity = keep.tile([P, P], F32, name="identity")
        make_identity(nc, identity[:])
        point_five = keep.tile([P, 1], F32, name="point_five")
        nc.gpsimd.memset(point_five[:], 0.5)

        def gather_packed(name, table, list_tile, dtype):
            tile = keep.tile([P, S], dtype, name=name, align_bytes=64)
            nc.vector.tensor_copy(tile[:], table[:].indirect(list_tile[:]))
            return tile

        key_bytes = gather_packed("key_bytes", d_byte_table, k1_list, U8)
        key_bytes_dealt = keep.tile([P, H], U8, name="key_bytes_dealt", align_bytes=64)
        nc.vector.tensor_copy(
            key_bytes_dealt[:].rearrange("p (t m) -> p t m", t=PACK),
            key_bytes[:].rearrange("p (m t) -> p t m", t=PACK),
        )
        for r in range(4):
            source = D_SCALE_STEP * r
            nc.sync.dma_start(
                key_scales[r:P:QUADRANT, :].bitcast(I32), key_bytes_dealt[source:P:QUADRANT, :].bitcast(I32)
            )
        key_words = gather_packed("key_words", d_word_table, k1_list, U32)
        key_codes = keep.tile([P, H], U32, name="key_codes", align_bytes=64)
        nc.vector.tensor_copy(
            key_codes[:].rearrange("p (t m) -> p m t", t=PACK),
            key_words[:].rearrange("p (m t) -> p m t", t=PACK),
        )
        b_scales = gather_packed("b_scales", x_byte_table, two_list, U8)
        a_scales = gather_packed("a_scales", x_byte_table, offs_list, U8)
        b_codes = gather_packed("b_codes", x_word_table, two_list, U32)
        a_codes = gather_packed("a_codes", x_word_table, offs_list, U32)

        def product(result_bank, t, lhs_codes, lhs_scales, rhs_codes, rhs_scales, cols):
            rows = slice(t * P, (t + 1) * P)
            nc.tensor.matmul_mx(
                out=result_bank[:, cols],
                lhsT=lhs_codes[:, rows].bitcast(FP8X4),
                lhsT_scale=lhs_scales[:, rows],
                rhs=rhs_codes[:, cols].bitcast(FP8X4),
                rhs_scale=rhs_scales[:, cols],
                start=True,
                stop=True,
            )

        b_banks = [bank(f"b{t}", t) for t in range(PACK)]
        a_banks = [bank(f"a{t}", PACK + t) for t in range(PACK)]
        for t in range(PACK):
            product(b_banks[t], t, key_codes, key_scales, b_codes, b_scales[X_SCALE_ROW:, :], ALL)
        for t in range(PACK):
            product(a_banks[t], t, key_codes, key_scales, a_codes, a_scales[X_SCALE_ROW:, :], ALL)

        z_rows = keep.tile([P, PACK, S], BF16, name="z_rows", align_bytes=64)
        w_grouped = keep.tile([P, N * PACK], BF16, name="w_grouped", align_bytes=64)
        w_codes = keep.tile([P, N], U32, name="w_codes", align_bytes=64)
        w_scales = keep.tile([P, N], U8, name="w_scales", align_bytes=64)
        z_grouped = keep.tile([P, S, PACK], BF16, name="z_grouped", align_bytes=64)
        z_codes = keep.tile([P, S], U32, name="z_codes", align_bytes=64)
        z_scales = keep.tile([P, S], U8, name="z_scales", align_bytes=64)
        b_windows = row_tiles("b_window")
        minus_b2 = row_tiles("minus_b2_")
        diff = row_tiles("diff")
        squash = row_tiles("squash")
        h_windows = row_tiles("h_window")
        partner = row_tiles("partner")
        h_sq = row_tiles("h_sq")
        partner_sq = row_tiles("partner_sq")
        root = row_tiles("root")
        inverse = row_tiles("inverse")
        numer = row_tiles("numer")
        result = row_tiles("result")
        unread = keep.tile([P, 1], F32, name="unread")

        w_dealt = w_grouped[:].rearrange("p (t m j) -> p m j t", t=PACK, j=PACK)
        for u in range(2):
            nc.scalar.copy(
                w_dealt[:, u * P // 2 : (u + 1) * P // 2], w_halves[u][:].rearrange("p j (m t) -> p m j t", t=PACK)
            )
        nc.vector.quantize_mx(out=w_codes[:].bitcast(FP8X4), scales=w_scales[:], in_=w_grouped[:])

        def copy_b(t):
            if t in B_COPIES_ON_VECTOR:
                nc.vector.tensor_copy(b_windows[t][:], b_banks[t][:])
            else:
                nc.scalar.copy(b_windows[t][:], b_banks[t][:])

        def fetch_b2(t, cols):
            window = b_windows[t][:].indirect(entries(n2_list, cols))
            nc.scalar.activation(minus_b2[t][:, cols], window, ACT.Copy, scale=-1.0)

        def fetch_b1(t, cols):
            window = b_windows[t][:].indirect(entries(n1_list, cols))
            nc.vector.tensor_tensor(diff[t][:, cols], window, minus_b2[t][:, cols], ALU.add)

        def tanh(t, cols):
            nc.scalar.activation(squash[t][:, cols], diff[t][:, cols], ACT.Tanh, scale=0.0625)

        def gate(t, cols):
            nc.vector.scalar_tensor_tensor(
                z_rows[:, t, cols], a_banks[t][:, cols], gain16[:, t : t + 1], squash[t][:, cols], ALU.mult, ALU.mult
            )

        def quantize_z(cols):
            nc.vector.tensor_copy(
                z_grouped[:, cols, :].rearrange("p (c i) t -> p c t i", i=4),
                z_rows[:, :, cols].rearrange("p t (c i) -> p c t i", i=4),
            )
            nc.vector.quantize_mx(
                out=z_codes[:, cols].bitcast(FP8X4),
                scales=z_scales[:, cols],
                in_=z_grouped[:, cols, :].rearrange("p j t -> p (j t)"),
            )

        def square_h(t, cols):
            nc.scalar.activation(h_sq[t][:, cols], h_windows[t][:, cols], ACT.Square)

        pieces = [(t, cols) for cols in (FIRST, SECOND) for t in range(PACK)]
        stages = ((gate, GATE_LAG), (tanh, TANH_LAG), (fetch_b1, 1), (fetch_b2, 0))
        first_gated = LAST + GATE_LAG
        h_banks = []
        copy_b(0)
        for step in range(len(pieces) + GATE_LAG):
            for stage, lag in stages:
                if 0 <= step - lag < len(pieces):
                    stage(*pieces[step - lag])
                if step == first_gated and stage is gate:
                    quantize_z(FIRST)
                    for t in range(PACK):
                        h_banks.append(bank(f"h{t}", t))
                        product(h_banks[t], t, w_codes, w_scales, z_codes, z_scales, FIRST)
            if step + 1 < PACK:
                copy_b(step + 1)
            if 1 <= step - first_gated <= 2:
                for t in (2 * (step - first_gated) - 2, 2 * (step - first_gated) - 1):
                    nc.scalar.copy(h_windows[t][:, FIRST], h_banks[t][:, FIRST])
        for t in range(PACK):
            if t not in FIRST_SQUARES_ON_VECTOR:
                square_h(t, FIRST)
        nc.scalar.activation(
            unread[:], squash[LAST][:, S - 1 : S], ACT.Abs_reciprocal_sqrt, bias=point_five[:], scale=0.25
        )
        quantize_z(SECOND)
        for t in FIRST_SQUARES_ON_VECTOR:
            nc.vector.tensor_tensor(h_sq[t][:, FIRST], h_windows[t][:, FIRST], h_windows[t][:, FIRST], ALU.mult)
        for t in range(PACK):
            product(h_banks[t], t, w_codes, w_scales, z_codes, z_scales, SECOND)
        for t in range(PACK):
            nc.scalar.copy(h_windows[t][:, SECOND], h_banks[t][:, SECOND])

        out_rows = out.rearrange("(p t) j -> p t j", t=PACK)

        def turn(target_bank, sources, cols):
            blocks = [(source, c) for source in sources for c in range(cols.start, cols.stop, P)]
            for n, (source, c) in enumerate(blocks):
                nc.tensor.matmul(
                    target_bank[:, c : c + P],
                    lhsT=source[:, c : c + P],
                    rhs=identity[:],
                    is_transpose=True,
                    start=n == 0 or len(sources) == 1,
                    stop=n == len(blocks) - 1 or len(sources) == 1,
                )

        def fetch_partner(t):
            for cols in (FIRST, SECOND):
                nc.vector.tensor_copy(partner[t][:, cols], h_windows[t][:].indirect(entries(n3_list, cols)))
            square_h(t, SECOND)

        def square_partner(t):
            nc.scalar.activation(partner_sq[t][:], partner[t][:], ACT.Square)

        def inverse_root(t):
            turned = bank(f"turned{t}", PACK + t)
            turn(turned, (h_sq[t], partner_sq[t]), ALL)
            nc.scalar.activation(root[t][:], turned[:], ACT.Abs_reciprocal_sqrt, bias=point_five[:])

        def square_root(t, cols):
            nc.scalar.activation(inverse[t][:, cols], root[t][:, cols], ACT.Square)

        def finish(t, cols, number):
            back = bank(f"back{t}_{cols.start}", number)
            turn(back, (inverse[t],), cols)
            nc.vector.scalar_tensor_tensor(
                result[t][:, cols], numer[t][:, cols], 2.0, back[:, cols], ALU.mult, ALU.mult
            )
            nc.sync.dma_start(out_rows[:, t, cols], result[t][:, cols])

        for step in range(PACK + 3):
            if step < PACK:
                fetch_partner(step)
            if 0 <= step - 1 < PACK:
                square_partner(step - 1)
            if step - 2 == LAST:
                square_root(LAST - 1, ALL)
            if 0 <= step - 2 < PACK:
                inverse_root(step - 2)
            t = step - 3
            if t >= 0:
                nc.vector.tensor_tensor(numer[t][:], h_banks[t][:], partner[t][:], ALU.mult)
            if 0 <= t < LAST:
                if t != LAST - 1:
                    square_root(t, ALL)
                finish(t, ALL, t)
            if t == LAST:
                for cols, number in ((FIRST, LAST), (SECOND, 0)):
                    square_root(t, cols)
                    finish(t, cols, number)
